import numpy as np, ml_dtypes
CORES = [242,247,114,119]
N = 4
TK = 128
COEF = [[2,-1,1,-1],[-1,2,-1,1],[1,-1,2,-1],[-1,1,-1,2]]
def setup_inputs(rng):
    return {"x": rng.standard_normal((N, 128, TK), dtype=np.float32).astype(ml_dtypes.bfloat16), "a": (rng.standard_normal((N, 128, 128), dtype=np.float32) / 11).astype(ml_dtypes.bfloat16)}
def setup_inputs_big(rng):
    d = setup_inputs(rng)
    for k in ("x", "a"): d[k] = (d[k].astype(np.float32) * 1024.0).astype(d[k].dtype)
    return d
def setup_inputs_small(rng):
    d = setup_inputs(rng)
    for k in ("x", "a"): d[k] = (d[k].astype(np.float32) * (1 / 1024.0)).astype(d[k].dtype)
    return d
def setup_inputs_apart(rng):
    d = setup_inputs(rng)
    f = (10.0 ** rng.permutation(np.linspace(-1.5, 1.5, N))).astype(np.float32).reshape(N, 1, 1)
    for k in ("x", "a"): d[k] = (d[k].astype(np.float32) * f).astype(d[k].dtype)
    return d
def reference(x, a):
    X, A = x.astype(np.float64), a.astype(np.float64)
    y = np.stack([A[r].T @ sum(COEF[r][j] * X[j] for j in range(N)) for r in range(N)])
    return {"y": y.astype(ml_dtypes.bfloat16)}

from concourse.bass import DstId, RemoteDMATransfer
from concourse.mybir import AluOpType

_N = 4
SCRATCH = {
    "xd": ("dram", [128, 128], "bfloat16"),
    "xs": ("sbuf", [128, 128], "bfloat16"),
    "a1": ("sbuf", [128, 128], "bfloat16"),
    "ps": ("psum", [128, 128], "float32"),
    "ys": ("sbuf", [128, 128], "bfloat16"),
}
for _j in range(_N):
    SCRATCH["land%d" % _j] = ("sbuf", [128, 128], "bfloat16")
    SCRATCH["ac%d" % _j] = ("sbuf", [128, 128], "bfloat16")
    SCRATCH["cc%d" % _j] = ("sbuf", [128, 128], "bfloat16")
SEMAPHORES = ["ld_xd", "ld_xs", "ld_a", "cst", "scl", "mm", "cp", "st", "sent"] + ["arr%d" % _j for _j in range(_N)]


def _bits(m):
    return [b for b in range(m.bit_length()) if (m >> b) & 1]


def _mask(engs):
    m = 0
    for b in engs:
        m |= 1 << b
    return m


def _share(engs, n):
    size = 1
    while size * 2 * n <= len(engs):
        size *= 2
    return [engs[i * size:(i + 1) * size] for i in range(n)]


def _plan(src, T, topo):
    coef = T.tables["COEF"]
    j = T.rank_of(src)
    dsts = [d for r, d in enumerate(T.cores) if d != src and coef[r][j] != 0]
    here = (topo.host(src), topo.chip(src))
    near = [d for d in dsts if (topo.host(d), topo.chip(d)) == here]
    far = [d for d in dsts if (topo.host(d), topo.chip(d)) != here]
    calls, used = [], []
    if far:
        m = -1
        for d in far:
            m &= topo.mask(src, d)
        groups = _share(_bits(m), len(far))
        calls.append(list(zip(far, groups)))
        used = [b for grp in groups for b in grp]
    if near:
        m = -1
        for d in near:
            m &= topo.mask(src, d)
        free = [b for b in _bits(m) if b not in used]
        calls.append(list(zip(near, _share(free if len(free) >= len(near) else _bits(m), len(near)))))
    return calls


def rank_program(g, core, T, topo):
    rank = T.rank_of(core)
    if rank is None:
        return
    S = T.sem
    w = T.tables["COEF"][rank]

    g.sync.dma_start(T.xd[:], T.x[:]).then_inc(S.ld_xd, 16)
    g.sync.dma_start(T.a1[:], T.a[:]).then_inc(S.ld_a, 16)
    g.sync.dma_start(T.xs[:], T.x[:]).then_inc(S.ld_xs, 16)

    g.wait_ge(S.ld_xd, 16)
    sent = 0
    for call in _plan(core, T, topo):
        trs = []
        for d, engs in call:
            rid, pid = topo.addr(d, core)
            trs.append(RemoteDMATransfer(dst_ids=[DstId(rid=rid, pnc=pid)], dma_engine_mask=_mask(engs),
                                         remote_sem=S["arr%d" % rank], src=T.xd[:], dst=T["land%d" % rank][:]))
            sent += len(engs)
        g.remote_dma_fused(trs, local_sem=S.sent)

    vals = sorted(set(c for c in w if c not in (0, 1)))
    lhs = {1: T.a1}
    for k, c in enumerate(vals):
        g.vector.memset(T["cc%d" % k][:], float(c)).then_inc(S.cst, 1)
        lhs[c] = T["ac%d" % k]
    if vals:
        g.vector.wait_ge(S.cst, len(vals))
        g.vector.wait_ge(S.ld_a, 16)
    for k, c in enumerate(vals):
        g.vector.tensor_tensor(T["ac%d" % k][:], T.a1[:], T["cc%d" % k][:], AluOpType.mult).then_inc(S.scl, 1)

    terms = []
    if w[rank] != 0:
        terms.append((S.ld_xs, 16, T.xs, w[rank]))
    arrivals = []
    for j, s in enumerate(T.cores):
        if s == core or w[j] == 0:
            continue
        for pos, call in enumerate(_plan(s, T, topo)):
            for d, engs in call:
                if d == core:
                    same = (topo.host(s), topo.chip(s)) == (topo.host(core), topo.chip(core))
                    arrivals.append((0 if same else 1, j, len(engs)))
    for _, j, n in sorted(arrivals):
        terms.append((S["arr%d" % j], n, T["land%d" % j], w[j]))
    g.tensor.wait_ge(S.ld_a, 16)
    if vals:
        g.tensor.wait_ge(S.scl, len(vals))
    if w[rank] == 0:
        g.tensor.wait_ge(S.ld_xs, 16)
    for i, (sem, n, rhs, c) in enumerate(terms):
        g.tensor.wait_ge(sem, n)
        mmi = g.tensor.matmul(T.ps[:], lhs[c][:], rhs[:], i == 0, i == len(terms) - 1)
    mmi.then_inc(S.mm, 1)

    g.vector.wait_ge(S.mm, 1)
    g.vector.tensor_copy(T.ys[:], T.ps[:]).then_inc(S.cp, 1)
    g.scalar.wait_ge(S.cp, 1)
    g.scalar.dma_start(T.y[:], T.ys[:]).then_inc(S.st, 16)
    g.scalar.wait_ge(S.st, 16)
    g.wait_ge(S.sent, sent)
